import numpy as np, ml_dtypes
CORES = [51,54,179,182]
N = 4
import mx_ref
NC, G, D = 128, 4, 8
C = np.float32(0.047)
BF = ml_dtypes.bfloat16
def cut(t, i, w=512):
    return t[:, w * i:w * i + w]
def tile(rs):
    return np.stack(rs, axis=2).reshape(128, -1).astype(BF)
def act(Z):
    return [np.maximum(z, 0) * C for z in Z]
def taps(w, i, e):
    return mx_ref.matmul(mx_ref.quantize(cut(w, 2 * i)), mx_ref.quantize(e[:, :4 * NC])) + mx_ref.matmul(mx_ref.quantize(cut(w, 2 * i + 1)), mx_ref.quantize(e[:, 4 * D:4 * D + 4 * NC]))
def setup_inputs(rng):
    def f(*shape):
        return mx_ref.flush((rng.standard_normal(shape, dtype=np.float32) * np.exp2(rng.integers(-2, 3, shape[:-1] + (1,)))).astype(BF))
    return {"x": f(N, 128, 4 * NC), "wa": np.broadcast_to(f(1, 128, 2 * G * 512), (N, 128, 2 * G * 512)).copy(), "wb": f(N, 128, 2 * 512)}
def setup_inputs_blocks(rng):
    d = setup_inputs(rng)
    for k in ("x", "wb"): d[k] = mx_ref.spread(d[k], rng, 2)
    return d
def setup_inputs_wide(rng):
    d = setup_inputs(rng)
    for k in ("wb",): d[k] = mx_ref.flush((d[k].astype(np.float32) * np.exp2(rng.integers(-6, 7, (N, 1, 1))).astype(np.float32)).astype(BF))
    return d
def setup_inputs_zeros(rng):
    d = setup_inputs(rng); v = d["x"].reshape(N, 128, -1, 4).copy()
    v[np.broadcast_to((rng.random((N, 1, v.shape[2], 1)) < 0.33), v.shape)] = 0
    d["x"] = v.reshape(d["x"].shape)
    return d
def reference(x, wa, wb):
    edge = lambda t, r: np.concatenate([t[(r - 1) % N][:, 4 * (NC - D):], t[r]], axis=1)
    u = [tile(act([taps(wa[r], i, edge(x, r)) for i in range(G)])) for r in range(N)]
    y = np.zeros((N, 128, NC), np.float32)
    for r in range(N):
        y[r] = taps(wb[r], 0, edge(u, r))
    return {"y": y}

@@ -1,0 +1,100 @@
+from concourse.mybir import dt, ActivationFunctionType
+
+NC, G, D = 128, 4, 8
+H = 2 * D
+E1 = H + NC
+E2 = D + NC
+TW = 4 * NC
+HALF = 4
+ENGINES = 8
+
+SCRATCH = {
+    "xb": ("sbuf", [128, TW], "bfloat16"),
+    "wab": ("sbuf", [128, 2 * G * TW], "bfloat16"),
+    "wbb": ("sbuf", [128, 2 * TW], "bfloat16"),
+    "ub": ("sbuf", [128, 4 * E2], "bfloat16"),
+    "yb": ("sbuf", [128, NC], "float32"),
+    "xq": ("sbuf", [128, E1], "float8_e4m3fn_x4"),
+    "xs": ("sbuf", [128, E1], "uint8"),
+    "aq": ("sbuf", [128, 2 * G * NC], "float8_e4m3fn_x4"),
+    "as_": ("sbuf", [128, 2 * G * NC], "uint8"),
+    "bq": ("sbuf", [128, 2 * NC], "float8_e4m3fn_x4"),
+    "bs": ("sbuf", [128, 2 * NC], "uint8"),
+    "uq": ("sbuf", [128, E2], "float8_e4m3fn_x4"),
+    "us": ("sbuf", [128, E2], "uint8"),
+    "zp": ("psum", [128, 512 * G], "float32"),
+    "yp": ("psum", [128, 512], "float32"),
+}
+SEMAPHORES = (["ld_x", "ld_b", "qx", "act", "qu", "yz", "yc", "stored", "halo", "sent"] + ["ld_a%d" % h for h in range(2 * G // HALF)]
+              + ["qa%d" % k for k in range(2 * G)] + ["qb%d" % t for t in range(2)] + ["z%d" % i for i in range(G)])
+
+
+def lowest(mask, n):
+    out = 0
+    while n:
+        bit = mask & -mask
+        out, mask, n = out | bit, mask ^ bit, n - 1
+    return out
+
+
+def rank_program(g, core, T, topo):
+    rank = T.rank_of(core)
+    if rank is None:
+        return
+    s = T.sem
+    nxt = T.cores[(rank + 1) % len(T.cores)]
+    col = lambda k: slice(NC * k, NC * k + NC)
+    elt = lambda k, n=1: slice(TW * k, TW * (k + n))
+
+    g.sync.dma_start(T.xb[:], T.x[:]).then_inc(s.ld_x, 16)
+    for h in range(2 * G // HALF):
+        g.sync.dma_start(T.wab[:, elt(HALF * h, HALF)], T.wa[:, elt(HALF * h, HALF)]).then_inc(s["ld_a%d" % h], 16)
+    g.sync.dma_start(T.wbb[:], T.wb[:]).then_inc(s.ld_b, 16)
+
+    g.vector.wait_ge(s.ld_x, 16)
+    g.vector.quantize_mx(T.xq[:, H:E1], T.xs[:, H:E1], T.xb[:]).then_inc(s.qx, 1)
+    for k in range(2 * G):
+        if k % HALF == 0:
+            g.vector.wait_ge(s["ld_a%d" % (k // HALF)], 16)
+        g.vector.quantize_mx(T.aq[:, col(k)], T.as_[:, col(k)], T.wab[:, elt(k)]).then_inc(s["qa%d" % k], 1)
+
+    rid, pid = topo.addr(nxt, core)
+    mask = lowest(topo.mask(core, nxt), ENGINES)
+    g.wait_ge(s.qx, 1)
+    g.remote_dma(T.xq[:, 0:H].bitcast(dt.uint8), T.xq[:, NC:E1].bitcast(dt.uint8), s.halo, s.sent, pid, rid, mask)
+    g.remote_dma(T.xs[:, 0:H], T.xs[:, NC:E1], s.halo, s.sent, pid, rid, mask)
+    g.wait_ge(s.sent, 2 * ENGINES)
+
+    g.tensor.wait_ge(s.qx, 1)
+    g.tensor.wait_ge(s.halo, 2 * ENGINES)
+    for i in range(G):
+        for t in range(2):
+            k = 2 * i + t
+            g.tensor.wait_ge(s["qa%d" % k], 1)
+            m = g.tensor.matmul_mx(T.zp[:, 512 * i:512 * i + E2], T.aq[:, col(k)], T.as_[:, col(k)],
+                                   T.xq[:, D * t:D * t + E2], T.xs[:, D * t:D * t + E2], t == 0, t == 1)
+        m.then_inc(s["z%d" % i], 1)
+
+    for i in range(G):
+        g.scalar.wait_ge(s["z%d" % i], 1)
+        g.scalar.activation(T.ub[:, i:4 * E2:4], T.zp[:, 512 * i:512 * i + E2], ActivationFunctionType.Relu,
+                            scale=0.047).then_inc(s.act, 1)
+
+    g.vector.wait_ge(s.ld_b, 16)
+    g.vector.quantize_mx(T.bq[:, col(0)], T.bs[:, col(0)], T.wbb[:, elt(0)]).then_inc(s.qb0, 1)
+    g.vector.wait_ge(s.act, G)
+    g.vector.quantize_mx(T.uq[:], T.us[:], T.ub[:]).then_inc(s.qu, 1)
+    g.vector.quantize_mx(T.bq[:, col(1)], T.bs[:, col(1)], T.wbb[:, elt(1)]).then_inc(s.qb1, 1)
+
+    g.tensor.wait_ge(s.qu, 1)
+    for t in range(2):
+        g.tensor.wait_ge(s["qb%d" % t], 1)
+        m = g.tensor.matmul_mx(T.yp[:, 0:NC], T.bq[:, col(t)], T.bs[:, col(t)],
+                               T.uq[:, D * t:D * t + NC], T.us[:, D * t:D * t + NC], t == 0, t == 1)
+    m.then_inc(s.yz, 1)
+
+    g.vector.wait_ge(s.yz, 1)
+    g.vector.tensor_copy(T.yb[:], T.yp[:, 0:NC]).then_inc(s.yc, 1)
+    g.sync.wait_ge(s.yc, 1)
+    g.sync.dma_start(T.y[:], T.yb[:]).then_inc(s.stored, 16)
+    g.sync.wait_ge(s.stored, 16)

@@ -4,29 +4,39 @@ NC, G, D = 128, 4, 8
 H = 2 * D
 E1 = H + NC
 E2 = D + NC
+EU = H + D
 TW = 4 * NC
-HALF = 4
+LOADS = (3, 3, 2)
 ENGINES = 8
+BANK = 512
 
 SCRATCH = {
     "xb": ("sbuf", [128, TW], "bfloat16"),
     "wab": ("sbuf", [128, 2 * G * TW], "bfloat16"),
     "wbb": ("sbuf", [128, 2 * TW], "bfloat16"),
     "ub": ("sbuf", [128, 4 * E2], "bfloat16"),
-    "yb": ("sbuf", [128, NC], "float32"),
+    "ue": ("sbuf", [128, 4 * E2], "bfloat16"),
+    "yb": ("sbuf", [128, NC - H], "float32"),
+    "ye": ("sbuf", [128, H], "float32"),
     "xq": ("sbuf", [128, E1], "float8_e4m3fn_x4"),
     "xs": ("sbuf", [128, E1], "uint8"),
+    "vq": ("sbuf", [128, E1], "float8_e4m3fn_x4"),
+    "vs": ("sbuf", [128, E1], "uint8"),
     "aq": ("sbuf", [128, 2 * G * NC], "float8_e4m3fn_x4"),
     "as_": ("sbuf", [128, 2 * G * NC], "uint8"),
     "bq": ("sbuf", [128, 2 * NC], "float8_e4m3fn_x4"),
     "bs": ("sbuf", [128, 2 * NC], "uint8"),
-    "uq": ("sbuf", [128, E2], "float8_e4m3fn_x4"),
-    "us": ("sbuf", [128, E2], "uint8"),
-    "zp": ("psum", [128, 512 * G], "float32"),
-    "yp": ("psum", [128, 512], "float32"),
+    "ubq": ("sbuf", [128, E2], "float8_e4m3fn_x4"),
+    "ubs": ("sbuf", [128, E2], "uint8"),
+    "ueq": ("sbuf", [128, E2], "float8_e4m3fn_x4"),
+    "ues": ("sbuf", [128, E2], "uint8"),
+    "zb": ("psum", [128, BANK * G], "float32"),
+    "ze": ("psum", [128, BANK * G], "float32"),
 }
-SEMAPHORES = (["ld_x", "ld_b", "qx", "act", "qu", "yz", "yc", "stored", "halo", "sent"] + ["ld_a%d" % h for h in range(2 * G // HALF)]
-              + ["qa%d" % k for k in range(2 * G)] + ["qb%d" % t for t in range(2)] + ["z%d" % i for i in range(G)])
+SEMAPHORES = (["fill", "ld_x", "ld_b", "qx", "qv0", "qv", "actb", "acte", "qub", "que", "yzb", "yze", "ycb", "yce", "st_b", "st_e", "halo",
+               "sent"]
+              + ["ld_a%d" % h for h in range(len(LOADS))] + ["qa%d" % k for k in range(2 * G)] + ["qb%d" % t for t in range(2)]
+              + ["zb%d" % i for i in range(G)] + ["ze%d" % i for i in range(G)])
 
 
 def lowest(mask, n):
@@ -45,18 +55,27 @@ def rank_program(g, core, T, topo):
     nxt = T.cores[(rank + 1) % len(T.cores)]
     col = lambda k: slice(NC * k, NC * k + NC)
     elt = lambda k, n=1: slice(TW * k, TW * (k + n))
+    first = [sum(LOADS[:h]) for h in range(len(LOADS))]
 
     g.sync.dma_start(T.xb[:], T.x[:]).then_inc(s.ld_x, 16)
-    for h in range(2 * G // HALF):
-        g.sync.dma_start(T.wab[:, elt(HALF * h, HALF)], T.wa[:, elt(HALF * h, HALF)]).then_inc(s["ld_a%d" % h], 16)
+    for h, n in enumerate(LOADS):
+        g.sync.dma_start(T.wab[:, elt(first[h], n)], T.wa[:, elt(first[h], n)]).then_inc(s["ld_a%d" % h], 16)
+    g.sync.wait_ge(s.ld_a0, 16)
     g.sync.dma_start(T.wbb[:], T.wb[:]).then_inc(s.ld_b, 16)
 
+    g.vector.memset(T.ue[:, 4 * EU:4 * E2], 0.0).then_inc(s.fill, 1)
     g.vector.wait_ge(s.ld_x, 16)
     g.vector.quantize_mx(T.xq[:, H:E1], T.xs[:, H:E1], T.xb[:]).then_inc(s.qx, 1)
+    g.vector.quantize_mx(T.vq[:, H:E1], T.vs[:, H:E1], T.xb[:]).then_inc(s.qv0, 1)
+    g.vector.wait_ge(s.qv0, 1)
+    g.vector.quantize_mx(T.vq[:, 0:NC], T.vs[:, 0:NC], T.xb[:]).then_inc(s.qv, 1)
     for k in range(2 * G):
-        if k % HALF == 0:
-            g.vector.wait_ge(s["ld_a%d" % (k // HALF)], 16)
+        if k in first:
+            g.vector.wait_ge(s["ld_a%d" % first.index(k)], 16)
         g.vector.quantize_mx(T.aq[:, col(k)], T.as_[:, col(k)], T.wab[:, elt(k)]).then_inc(s["qa%d" % k], 1)
+    g.vector.wait_ge(s.ld_b, 16)
+    for t in range(2):
+        g.vector.quantize_mx(T.bq[:, col(t)], T.bs[:, col(t)], T.wbb[:, elt(t)]).then_inc(s["qb%d" % t], 1)
 
     rid, pid = topo.addr(nxt, core)
     mask = lowest(topo.mask(core, nxt), ENGINES)
@@ -65,36 +84,54 @@ def rank_program(g, core, T, topo):
     g.remote_dma(T.xs[:, 0:H], T.xs[:, NC:E1], s.halo, s.sent, pid, rid, mask)
     g.wait_ge(s.sent, 2 * ENGINES)
 
+    def layer1(z, name, q, p, width):
+        for i in range(G):
+            for t in range(2):
+                k = 2 * i + t
+                g.tensor.wait_ge(s["qa%d" % k], 1)
+                m = g.tensor.matmul_mx(z[:, BANK * i:BANK * i + width], T.aq[:, col(k)], T.as_[:, col(k)],
+                                       q[:, D * t:D * t + width], p[:, D * t:D * t + width], t == 0, t == 1)
+            m.then_inc(s["%s%d" % (name, i)], 1)
+
+    def steps(z, name, u, width, done):
+        for i in range(G):
+            g.scalar.wait_ge(s["%s%d" % (name, i)], 1)
+            g.scalar.activation(u[:, i:4 * width:4], z[:, BANK * i:BANK * i + width], ActivationFunctionType.Relu,
+                                scale=0.047).then_inc(done, 1)
+
+    def layer2(bank, q, p, done):
+        for t in range(2):
+            g.tensor.wait_ge(s["qb%d" % t], 1)
+            m = g.tensor.matmul_mx(T.zb[:, BANK * bank:BANK * bank + NC], T.bq[:, col(t)], T.bs[:, col(t)],
+                                   q[:, D * t:D * t + NC], p[:, D * t:D * t + NC], t == 0, t == 1)
+        m.then_inc(done, 1)
+
+    g.tensor.wait_ge(s.qv, 1)
+    layer1(T.zb, "zb", T.vq, T.vs, E2)
+    steps(T.zb, "zb", T.ub, E2, s.actb)
     g.tensor.wait_ge(s.qx, 1)
     g.tensor.wait_ge(s.halo, 2 * ENGINES)
-    for i in range(G):
-        for t in range(2):
-            k = 2 * i + t
-            g.tensor.wait_ge(s["qa%d" % k], 1)
-            m = g.tensor.matmul_mx(T.zp[:, 512 * i:512 * i + E2], T.aq[:, col(k)], T.as_[:, col(k)],
-                                   T.xq[:, D * t:D * t + E2], T.xs[:, D * t:D * t + E2], t == 0, t == 1)
-        m.then_inc(s["z%d" % i], 1)
+    layer1(T.ze, "ze", T.xq, T.xs, NC)
+    steps(T.ze, "ze", T.ue, EU, s.acte)
 
-    for i in range(G):
-        g.scalar.wait_ge(s["z%d" % i], 1)
-        g.scalar.activation(T.ub[:, i:4 * E2:4], T.zp[:, 512 * i:512 * i + E2], ActivationFunctionType.Relu,
-                            scale=0.047).then_inc(s.act, 1)
+    g.vector.wait_ge(s.actb, G)
+    g.vector.quantize_mx(T.ubq[:], T.ubs[:], T.ub[:]).then_inc(s.qub, 1)
+    g.vector.wait_ge(s.fill, 1)
+    g.vector.wait_ge(s.acte, G)
+    g.vector.quantize_mx(T.ueq[:], T.ues[:], T.ue[:]).then_inc(s.que, 1)
 
-    g.vector.wait_ge(s.ld_b, 16)
-    g.vector.quantize_mx(T.bq[:, col(0)], T.bs[:, col(0)], T.wbb[:, elt(0)]).then_inc(s.qb0, 1)
-    g.vector.wait_ge(s.act, G)
-    g.vector.quantize_mx(T.uq[:], T.us[:], T.ub[:]).then_inc(s.qu, 1)
-    g.vector.quantize_mx(T.bq[:, col(1)], T.bs[:, col(1)], T.wbb[:, elt(1)]).then_inc(s.qb1, 1)
+    g.tensor.wait_ge(s.qub, 1)
+    layer2(0, T.ubq, T.ubs, s.yzb)
+    g.tensor.wait_ge(s.que, 1)
+    layer2(1, T.ueq, T.ues, s.yze)
 
-    g.tensor.wait_ge(s.qu, 1)
-    for t in range(2):
-        g.tensor.wait_ge(s["qb%d" % t], 1)
-        m = g.tensor.matmul_mx(T.yp[:, 0:NC], T.bq[:, col(t)], T.bs[:, col(t)],
-                               T.uq[:, D * t:D * t + NC], T.us[:, D * t:D * t + NC], t == 0, t == 1)
-    m.then_inc(s.yz, 1)
-
-    g.vector.wait_ge(s.yz, 1)
-    g.vector.tensor_copy(T.yb[:], T.yp[:, 0:NC]).then_inc(s.yc, 1)
-    g.sync.wait_ge(s.yc, 1)
-    g.sync.dma_start(T.y[:], T.yb[:]).then_inc(s.stored, 16)
-    g.sync.wait_ge(s.stored, 16)
+    g.vector.wait_ge(s.yzb, 1)
+    g.vector.tensor_copy(T.yb[:], T.zb[:, 0:NC - H]).then_inc(s.ycb, 1)
+    g.sync.wait_ge(s.ycb, 1)
+    g.sync.dma_start(T.y[:, H:NC], T.yb[:]).then_inc(s.st_b, 16)
+    g.scalar.wait_ge(s.yze, 1)
+    g.scalar.activation(T.ye[:], T.zb[:, BANK:BANK + H], ActivationFunctionType.Copy).then_inc(s.yce, 1)
+    g.scalar.wait_ge(s.yce, 1)
+    g.scalar.dma_start(T.y[:, 0:H], T.ye[:]).then_inc(s.st_e, 16)
+    g.sync.wait_ge(s.st_b, 16)
+    g.scalar.wait_ge(s.st_e, 16)

from concourse.mybir import dt, ActivationFunctionType

NC, G, D = 128, 4, 8
H = 2 * D
E1 = H + NC
E2 = D + NC
EU = H + D
TW = 4 * NC
LOADS = (3, 3, 2)
ENGINES = 8
BANK = 512

SCRATCH = {
    "xb": ("sbuf", [128, TW], "bfloat16"),
    "wab": ("sbuf", [128, 2 * G * TW], "bfloat16"),
    "wbb": ("sbuf", [128, 2 * TW], "bfloat16"),
    "ub": ("sbuf", [128, 4 * E2], "bfloat16"),
    "ue": ("sbuf", [128, 4 * E2], "bfloat16"),
    "yb": ("sbuf", [128, NC - H], "float32"),
    "ye": ("sbuf", [128, H], "float32"),
    "xq": ("sbuf", [128, E1], "float8_e4m3fn_x4"),
    "xs": ("sbuf", [128, E1], "uint8"),
    "vq": ("sbuf", [128, E1], "float8_e4m3fn_x4"),
    "vs": ("sbuf", [128, E1], "uint8"),
    "aq": ("sbuf", [128, 2 * G * NC], "float8_e4m3fn_x4"),
    "as_": ("sbuf", [128, 2 * G * NC], "uint8"),
    "bq": ("sbuf", [128, 2 * NC], "float8_e4m3fn_x4"),
    "bs": ("sbuf", [128, 2 * NC], "uint8"),
    "ubq": ("sbuf", [128, E2], "float8_e4m3fn_x4"),
    "ubs": ("sbuf", [128, E2], "uint8"),
    "ueq": ("sbuf", [128, E2], "float8_e4m3fn_x4"),
    "ues": ("sbuf", [128, E2], "uint8"),
    "zb": ("psum", [128, BANK * G], "float32"),
    "ze": ("psum", [128, BANK * G], "float32"),
}
SEMAPHORES = (["fill", "ld_x", "ld_b", "qx", "qv0", "qv", "actb", "acte", "qub", "que", "yzb", "yze", "ycb", "yce", "st_b", "st_e", "halo",
               "sent"]
              + ["ld_a%d" % h for h in range(len(LOADS))] + ["qa%d" % k for k in range(2 * G)] + ["qb%d" % t for t in range(2)]
              + ["zb%d" % i for i in range(G)] + ["ze%d" % i for i in range(G)])


def lowest(mask, n):
    out = 0
    while n:
        bit = mask & -mask
        out, mask, n = out | bit, mask ^ bit, n - 1
    return out


def rank_program(g, core, T, topo):
    rank = T.rank_of(core)
    if rank is None:
        return
    s = T.sem
    nxt = T.cores[(rank + 1) % len(T.cores)]
    col = lambda k: slice(NC * k, NC * k + NC)
    elt = lambda k, n=1: slice(TW * k, TW * (k + n))
    first = [sum(LOADS[:h]) for h in range(len(LOADS))]

    g.sync.dma_start(T.xb[:], T.x[:]).then_inc(s.ld_x, 16)
    for h, n in enumerate(LOADS):
        g.sync.dma_start(T.wab[:, elt(first[h], n)], T.wa[:, elt(first[h], n)]).then_inc(s["ld_a%d" % h], 16)
    g.sync.wait_ge(s.ld_a0, 16)
    g.sync.dma_start(T.wbb[:], T.wb[:]).then_inc(s.ld_b, 16)

    g.vector.memset(T.ue[:, 4 * EU:4 * E2], 0.0).then_inc(s.fill, 1)
    g.vector.wait_ge(s.ld_x, 16)
    g.vector.quantize_mx(T.xq[:, H:E1], T.xs[:, H:E1], T.xb[:]).then_inc(s.qx, 1)
    g.vector.quantize_mx(T.vq[:, H:E1], T.vs[:, H:E1], T.xb[:]).then_inc(s.qv0, 1)
    g.vector.wait_ge(s.qv0, 1)
    g.vector.quantize_mx(T.vq[:, 0:NC], T.vs[:, 0:NC], T.xb[:]).then_inc(s.qv, 1)
    for k in range(2 * G):
        if k in first:
            g.vector.wait_ge(s["ld_a%d" % first.index(k)], 16)
        g.vector.quantize_mx(T.aq[:, col(k)], T.as_[:, col(k)], T.wab[:, elt(k)]).then_inc(s["qa%d" % k], 1)
    g.vector.wait_ge(s.ld_b, 16)
    for t in range(2):
        g.vector.quantize_mx(T.bq[:, col(t)], T.bs[:, col(t)], T.wbb[:, elt(t)]).then_inc(s["qb%d" % t], 1)

    rid, pid = topo.addr(nxt, core)
    mask = lowest(topo.mask(core, nxt), ENGINES)
    g.wait_ge(s.qx, 1)
    g.remote_dma(T.xq[:, 0:H].bitcast(dt.uint8), T.xq[:, NC:E1].bitcast(dt.uint8), s.halo, s.sent, pid, rid, mask)
    g.remote_dma(T.xs[:, 0:H], T.xs[:, NC:E1], s.halo, s.sent, pid, rid, mask)
    g.wait_ge(s.sent, 2 * ENGINES)

    def layer1(z, name, q, p, width):
        for i in range(G):
            for t in range(2):
                k = 2 * i + t
                g.tensor.wait_ge(s["qa%d" % k], 1)
                m = g.tensor.matmul_mx(z[:, BANK * i:BANK * i + width], T.aq[:, col(k)], T.as_[:, col(k)],
                                       q[:, D * t:D * t + width], p[:, D * t:D * t + width], t == 0, t == 1)
            m.then_inc(s["%s%d" % (name, i)], 1)

    def steps(z, name, u, width, done):
        for i in range(G):
            g.scalar.wait_ge(s["%s%d" % (name, i)], 1)
            g.scalar.activation(u[:, i:4 * width:4], z[:, BANK * i:BANK * i + width], ActivationFunctionType.Relu,
                                scale=0.047).then_inc(done, 1)

    def layer2(bank, q, p, done):
        for t in range(2):
            g.tensor.wait_ge(s["qb%d" % t], 1)
            m = g.tensor.matmul_mx(T.zb[:, BANK * bank:BANK * bank + NC], T.bq[:, col(t)], T.bs[:, col(t)],
                                   q[:, D * t:D * t + NC], p[:, D * t:D * t + NC], t == 0, t == 1)
        m.then_inc(done, 1)

    g.tensor.wait_ge(s.qv, 1)
    layer1(T.zb, "zb", T.vq, T.vs, E2)
    steps(T.zb, "zb", T.ub, E2, s.actb)
    g.tensor.wait_ge(s.qx, 1)
    g.tensor.wait_ge(s.halo, 2 * ENGINES)
    layer1(T.ze, "ze", T.xq, T.xs, NC)
    steps(T.ze, "ze", T.ue, EU, s.acte)

    g.vector.wait_ge(s.actb, G)
    g.vector.quantize_mx(T.ubq[:], T.ubs[:], T.ub[:]).then_inc(s.qub, 1)
    g.vector.wait_ge(s.fill, 1)
    g.vector.wait_ge(s.acte, G)
    g.vector.quantize_mx(T.ueq[:], T.ues[:], T.ue[:]).then_inc(s.que, 1)

    g.tensor.wait_ge(s.qub, 1)
    layer2(0, T.ubq, T.ubs, s.yzb)
    g.tensor.wait_ge(s.que, 1)
    layer2(1, T.ueq, T.ues, s.yze)

    g.vector.wait_ge(s.yzb, 1)
    g.vector.tensor_copy(T.yb[:], T.zb[:, 0:NC - H]).then_inc(s.ycb, 1)
    g.sync.wait_ge(s.ycb, 1)
    g.sync.dma_start(T.y[:, H:NC], T.yb[:]).then_inc(s.st_b, 16)
    g.scalar.wait_ge(s.yze, 1)
    g.scalar.activation(T.ye[:], T.zb[:, BANK:BANK + H], ActivationFunctionType.Copy).then_inc(s.yce, 1)
    g.scalar.wait_ge(s.yce, 1)
    g.scalar.dma_start(T.y[:, 0:H], T.ye[:]).then_inc(s.st_e, 16)
    g.sync.wait_ge(s.st_b, 16)
    g.scalar.wait_ge(s.st_e, 16)
